import numpy as np
import ml_dtypes


def mxq(x, axis, fmt="e4m3"):
    dtype, down = {"e4m3": (ml_dtypes.float8_e4m3fn, 7), "e5m2": (ml_dtypes.float8_e5m2, 14)}[fmt]
    v = np.moveaxis(np.asarray(x, np.float32).astype(ml_dtypes.bfloat16).astype(np.float64), axis, -1)
    blocks = v.reshape(v.shape[:-1] + (-1, 32))
    amax = np.abs(blocks).max(-1, keepdims=True)
    byte = np.maximum(np.where(amax > 0, np.frexp(amax)[1] - 1 + 127, 0) - down, 1)
    scale = np.exp2(byte - 127.0)
    codes = (blocks / scale).astype(np.float32).astype(dtype).astype(np.float64)
    return np.moveaxis((codes * scale).reshape(v.shape), -1, axis)


WIDE = False


def mx_kscale(k):
    if not WIDE:
        return np.ones(k)
    levels = np.array([10, -10, 5, -5, 0])
    if k % 512:
        return np.exp2(np.random.permutation(np.resize(levels, k // 32))).repeat(32)
    a = np.empty((k // 512, 16))
    for p in range(k // 512):
        a[p, :8] = np.random.permutation(np.resize(levels, 8))
        for g in range(8):
            far = levels[np.abs(levels - a[p, g]) >= 10]
            a[p, g + 8] = far[np.random.randint(len(far))]
    return np.exp2(a.ravel()).repeat(32)


BF16 = ml_dtypes.bfloat16


def bf(x):
    return np.asarray(x, np.float32).astype(BF16)


def f64(x):
    return np.asarray(x).astype(np.float64)


H, T, E, L, S, DV = 2, 4096, 512, 128, 384, 256
N = L + S


def _softmax_last(x):
    m = np.max(x, axis=-1, keepdims=True)
    p = np.exp(x - m)
    return p / np.sum(p, axis=-1, keepdims=True)


def draw0():
    s, t = mx_kscale(E), mx_kscale(N)
    root_n = np.sqrt(N)
    return {"q": bf(np.random.standard_normal((H, T, E)) * 2.0 * s),
            "k": bf(np.random.standard_normal((H, N, E)) / s),
            "v": bf(np.random.standard_normal((H, N, DV)) * 4.0 / root_n / t[:, None]),
            "gate": bf(np.random.uniform(0.5, 1.5, H)),
            "c": bf(np.random.standard_normal((H, N)) * root_n * t)}


def core(q, k, v, gate, c):
    qq = mxq(f64(q), 2, "e4m3")
    kq = mxq(f64(k), 2, "e4m3")
    z = (qq @ kq.transpose(0, 2, 1)) / np.sqrt(E)
    ap = _softmax_last(z[:, :, :L])
    at = _softmax_last(z[:, :, L:])
    gp = np.tanh(f64(gate))[:, None, None] * ap
    a = np.concatenate([gp, at], axis=-1)
    b = a * f64(c)[:, None, :]
    return mxq(b, 2, "e4m3") @ mxq(f64(v), 1, "e4m3")


def e4m3fn_bytes(y):
    return np.clip(np.asarray(y, np.float64), -448.0, 448.0).astype(np.float32).astype(ml_dtypes.float8_e4m3fn).view(np.uint8)


def e4m3fn_values(b):
    return np.asarray(b, np.uint8).view(ml_dtypes.float8_e4m3fn).astype(np.float64)


def setup_inputs():
    d = draw0()
    x0 = np.asarray(d['q']).astype(np.float64)
    s = (np.max(np.abs(x0), axis=(0, 1), keepdims=True) / 448.0).astype(np.float32)
    out = {}
    for k, v in d.items():
        if k == 'q':
            out['q_bytes'] = e4m3fn_bytes(x0 / s.astype(np.float64))
            out['q_scale'] = s
        else:
            out[k] = v
    return out


def reference(q_bytes, q_scale, k, v, gate, c):
    return core(e4m3fn_values(q_bytes) * q_scale.astype(np.float64), k, v, gate, c)

@@ -1,0 +1,385 @@
+from contextlib import ExitStack
+
+import concourse.mybir as mybir
+from concourse.masks import make_identity
+
+H, T, E, L, S, DV = 2, 4096, 512, 128, 384, 256
+N = L + S
+P = 128
+FLOPS = 2 * H * T * N * (E + DV)
+
+F32 = mybir.dt.float32
+BF16 = mybir.dt.bfloat16
+U32 = mybir.dt.uint32
+U8 = mybir.dt.uint8
+FP8 = mybir.dt.float8_e4m3fn
+FP8X4 = mybir.dt.float8_e4m3fn_x4
+ALU = mybir.AluOpType
+ACTF = mybir.ActivationFunctionType
+AX = mybir.AxisListType
+
+TILES = 2
+PAIR = TILES * P
+PAIRS_PER_HEAD = T // PAIR
+PAIRS = H * PAIRS_PER_HEAD
+ROOT = 512.0 ** -0.5
+SEG = ((0, 64), (64, 256))
+
+
+def tile_llamaadaptergatedpromptattention_t_kernel(tc, q_bytes, q_scale, k, v, gate, c, out):
+    nc = tc.nc
+    with ExitStack() as ctx:
+        keep = ctx.enter_context(tc.tile_pool(name="keep", bufs=1))
+        work = ctx.enter_context(tc.tile_pool(name="work", bufs=5))
+        psum = ctx.enter_context(tc.psum_pool(name="psum", bufs=1))
+        ctx.enter_context(tc.manual_schedule())
+
+        ident = keep.tile([P, P], F32)
+        make_identity(nc, ident[:])
+
+        q_raw = keep.tile([P, PAIRS * TILES * E], U8, align_bytes=64)
+        qs = keep.tile([P, E], F32, align_bytes=64)
+        k_raw = keep.tile([P, H, 4, E], BF16, align_bytes=64)
+        v_raw = keep.tile([P, H, 4, DV], BF16, align_bytes=64)
+        c_raw = keep.tile([P, H, N], BF16, align_bytes=64)
+        g_raw = keep.tile([P, H], BF16, align_bytes=64)
+        q_view = q_bytes.rearrange("h (j p i) e -> p (h j) (i e)", p=P, i=TILES)
+        out_view = out.rearrange("h (j p i) d -> (h j) p i d", p=P, i=TILES)
+        row = TILES * E
+
+        def load_q(a, b):
+            nc.sync.dma_start(
+                out=q_raw[:, a * row : b * row].rearrange("p (j x) -> p j x", x=row),
+                in_=q_view[:, a:b, :],
+            )
+
+        load_q(0, 1)
+        nc.sync.dma_start(out=qs[:], in_=q_scale.rearrange("a b e -> (a b e)").partition_broadcast(P))
+        nc.sync.dma_start(out=k_raw[:, 0, :, :], in_=k[0].rearrange("(r j) e -> r j e", j=4))
+        load_q(1, 2)
+        nc.sync.dma_start(out=v_raw[:, 0, :, :], in_=v[0].rearrange("(p t) d -> p t d", t=4))
+        nc.sync.dma_start(out=g_raw[:], in_=gate.partition_broadcast(P))
+        nc.sync.dma_start(out=c_raw[:].rearrange("p h n -> p (h n)"), in_=c.rearrange("h n -> (h n)").partition_broadcast(P))
+        load_q(2, 4)
+        load_q(4, 8)
+        nc.sync.dma_start(out=k_raw[:, 1, :, :], in_=k[1].rearrange("(r j) e -> r j e", j=4))
+        nc.sync.dma_start(out=v_raw[:, 1, :, :], in_=v[1].rearrange("(p t) d -> p t d", t=4))
+        load_q(8, 16)
+        load_q(16, 24)
+        load_q(24, 32)
+
+        tg = keep.tile([P, H], F32)
+        gain = keep.tile([P, H, 2, 256], F32, align_bytes=64)
+        k_codes = keep.tile([P, H, N], U32, align_bytes=64)
+        k_scales = keep.tile([P, H, N], U8, align_bytes=64)
+        v_codes = keep.tile([P, H, DV], U32, align_bytes=64)
+        v_scales = keep.tile([P, H, DV], U8, align_bytes=64)
+
+        def k_transposes(h, w, bank):
+            ps = psum.tile([P, 2, 2, P], F32, name=bank, bufs=1)
+            for e in range(2):
+                words = k_raw[:, h, 2 * w + e, :].bitcast(F32)
+                for u in range(2):
+                    nc.tensor.transpose(ps[:, e, u, :], words[:, u : 256 : 2], ident[:])
+            return ps
+
+        def k_copy(h, w, ps, kg, engine):
+            engine(
+                out=kg[:, w].bitcast(F32).rearrange("p (r e u) -> p r e u", e=2, u=2),
+                in_=ps[:].rearrange("p e u r -> p r e u"),
+            )
+
+        def k_quant(h, kg):
+            nc.vector.quantize_mx(
+                out=k_codes[:, h, :].bitcast(FP8X4),
+                scales=k_scales[:, h, :],
+                in_=kg[:].rearrange("p w x -> p (w x)"),
+            )
+
+        def v_group(h):
+            vg = keep.tile([P, DV, 4], BF16, align_bytes=64, name="v_grouped%d" % h)
+            nc.vector.tensor_copy(out=vg[:], in_=v_raw[:, h].rearrange("p t d -> p d t"))
+            return vg
+
+        def v_quant(h, vg):
+            nc.vector.quantize_mx(
+                out=v_codes[:, h, :].bitcast(FP8X4),
+                scales=v_scales[:, h, :],
+                in_=vg[:].rearrange("p d t -> p (d t)"),
+            )
+
+        def gains(h):
+            src = c_raw[:, h, :].rearrange("p (x u e) -> p u x e", u=2, e=2)
+            dst = gain[:, h].rearrange("p u (x e) -> p u x e", e=2)
+            nc.gpsimd.tensor_scalar(
+                out=dst[:, :, 0:32, :], in0=src[:, :, 0:32, :], scalar1=tg[:, h : h + 1], scalar2=1.0,
+                op0=ALU.mult, op1=ALU.mult,
+            )
+            nc.gpsimd.tensor_scalar(
+                out=dst[:, :, 32:128, :], in0=src[:, :, 32:128, :], scalar1=1.0, scalar2=1.0,
+                op0=ALU.mult, op1=ALU.mult,
+            )
+
+        live = {}
+
+        def gain_flip(h):
+            ps = psum.tile([P, 4, P], F32, name="flip_q", bufs=1)
+            flat = gain[:, h].rearrange("p u x -> p (u x)")
+            for g in range(4):
+                nc.tensor.transpose(ps[:, g, :], flat[:, g * P : (g + 1) * P], ident[:])
+            gt = keep.tile([P, 4, P], F32, name="gain_turned%d" % h)
+            nc.scalar.copy(out=gt[:], in_=ps[:])
+            live["gt", h] = gt
+
+        def gain_to_psum(h):
+            cp = psum.tile([P, 2, 256], F32, name="c", bufs=1)
+            flat = cp[:].rearrange("p u x -> p (u x)")
+            for g in range(4):
+                nc.tensor.transpose(flat[:, g * P : (g + 1) * P], live["gt", h][:, g, :], ident[:])
+            live["c", h] = cp
+
+        def cast_q(j):
+            qc = work.tile([P, E], BF16, align_bytes=64, name="q_cast")
+            nc.scalar.copy(out=qc[:], in_=q_raw[:, j * row + E : (j + 1) * row].bitcast(FP8))
+            live["cast", j] = qc
+
+        def scale_q0(j):
+            q0 = work.tile([P, E], BF16, align_bytes=64, name="q_plain0")
+            nc.vector.tensor_tensor(
+                out=q0[:], in0=q_raw[:, j * row : j * row + E].bitcast(FP8), in1=qs[:], op=ALU.mult,
+            )
+            live["qb", j, 0] = q0
+
+        def hold(j):
+            held = work.tile([P, 1], BF16, name="held")
+            nc.gpsimd.tensor_scalar(
+                out=held[:], in0=live["qb", j, 0][:, 0:1], scalar1=1.0, scalar2=1.0, op0=ALU.mult, op1=ALU.mult
+            )
+
+        def scale_q1(j):
+            q1 = work.tile([P, E], BF16, align_bytes=64, name="q_plain1")
+            nc.gpsimd.tensor_tensor(out=q1[:], in0=live["cast", j][:], in1=qs[:], op=ALU.mult)
+            live["qb", j, 1] = q1
+
+        def flip_q(j):
+            ps = psum.tile([P, 2, 2, P], F32, name="flip_q", bufs=1)
+            for i in range(TILES):
+                words = live["qb", j, i][:].bitcast(F32)
+                for u in range(2):
+                    nc.tensor.transpose(ps[:, i, u, :], words[:, u : 256 : 2], ident[:])
+            live["tq", j] = ps
+
+        def copy_q(j):
+            qg = work.tile([P, PAIR * 4], BF16, align_bytes=64, name="q_grouped")
+            nc.scalar.copy(
+                out=qg[:].bitcast(F32).rearrange("p (i r u) -> p i r u", i=TILES, u=2),
+                in_=live["tq", j][:].rearrange("p i u r -> p i r u"),
+            )
+            live["qg", j] = qg
+
+        def quant_q(j):
+            codes = work.tile([P, PAIR], U32, align_bytes=64, name="q_codes")
+            scales = work.tile([P, PAIR], U8, align_bytes=64, name="q_scales")
+            nc.vector.quantize_mx(out=codes[:].bitcast(FP8X4), scales=scales[:], in_=live["qg", j][:])
+            live["qc", j] = (codes, scales)
+
+        def scores(j):
+            h = j // PAIRS_PER_HEAD
+            codes, scales = live["qc", j]
+            for i in range(TILES):
+                z = psum.tile([P, 2, 256], F32, name="z", bufs=4)
+                nc.tensor.matmul_mx(
+                    out=z[:].rearrange("p u x -> p (u x)"),
+                    lhsT=codes[:, i * P : (i + 1) * P].bitcast(FP8X4),
+                    lhsT_scale=scales[:, i * P : (i + 1) * P],
+                    rhs=k_codes[:, h, :].bitcast(FP8X4),
+                    rhs_scale=k_scales[:, h, :],
+                    start=True,
+                    stop=True,
+                )
+                live["z", j, i] = z
+
+        def maxima(j, i):
+            if i == 0:
+                live["m", j] = work.tile([P, 2 * TILES], F32, name="row_max")
+            m = live["m", j]
+            for s, (a, b) in enumerate(SEG):
+                nc.vector.tensor_reduce(
+                    out=m[:, 2 * i + s : 2 * i + s + 1], in_=live["z", j, i][:, :, a:b], axis=AX.XY, op=ALU.max
+                )
+
+        def biases(j):
+            nb = work.tile([P, 2 * TILES], F32, name="neg_max")
+            nc.gpsimd.tensor_scalar(
+                out=nb[:], in0=live["m", j][:], scalar1=-ROOT, scalar2=1.0, op0=ALU.mult, op1=ALU.mult
+            )
+            live["nb", j] = nb
+
+        def exps(j, i):
+            if ("sums", j) not in live:
+                live["sums", j] = work.tile([P, 2 * TILES], F32, name="row_sum")
+            sums = live["sums", j]
+            nb = live["nb", j]
+            ex = work.tile([P, 2, 256], F32, align_bytes=64, name="ex%d" % i)
+            for s, (a, b) in enumerate(SEG):
+                col = slice(2 * i + s, 2 * i + s + 1)
+                nc.scalar.activation(
+                    out=ex[:, :, a:b], in_=live["z", j, i][:, :, a:b], func=ACTF.Exp,
+                    bias=nb[:, col], scale=ROOT, accum_out=sums[:, col],
+                )
+            live["ex", j, i] = ex
+
+        def recips(j):
+            r = work.tile([P, 2 * TILES], F32, name="recip")
+            nc.vector.reciprocal(out=r[:], in_=live["sums", j][:])
+            live["r", j] = r
+
+        def norms(j, i):
+            h = j // PAIRS_PER_HEAD
+            bb = work.tile([P, 2, 256], BF16, align_bytes=64, name="b_plain%d" % i)
+            for s, (a, b) in enumerate(SEG):
+                nc.vector.scalar_tensor_tensor(
+                    out=bb[:, :, a:b], in0=live["ex", j, i][:, :, a:b],
+                    scalar=live["r", j][:, 2 * i + s : 2 * i + s + 1],
+                    in1=live["c", h][:, :, a:b], op0=ALU.mult, op1=ALU.mult,
+                )
+            live["bb", j, i] = bb
+
+        def flip_b(j):
+            ps = psum.tile([P, 2, 2, P], F32, name="flip_b", bufs=1)
+            for i in range(TILES):
+                words = live["bb", j, i][:].rearrange("p u x -> p (u x)").bitcast(F32)
+                for u in range(2):
+                    nc.tensor.transpose(ps[:, i, u, :], words[:, 128 * u : 128 * (u + 1)], ident[:])
+            live["tb", j] = ps
+
+        def copy_b(j):
+            bg = work.tile([P, PAIR * 4], BF16, align_bytes=64, name="b_grouped")
+            nc.scalar.copy(
+                out=bg[:].bitcast(F32).rearrange("p (i r u) -> p i r u", i=TILES, u=2),
+                in_=live["tb", j][:].rearrange("p i u r -> p i r u"),
+            )
+            live["bg", j] = bg
+
+        def quant_b(j):
+            codes = work.tile([P, PAIR], U32, align_bytes=64, name="b_codes")
+            scales = work.tile([P, PAIR], U8, align_bytes=64, name="b_scales")
+            nc.vector.quantize_mx(out=codes[:].bitcast(FP8X4), scales=scales[:], in_=live["bg", j][:])
+            live["bc", j] = (codes, scales)
+
+        def outputs(j):
+            h = j // PAIRS_PER_HEAD
+            codes, scales = live["bc", j]
+            o = psum.tile([P, TILES, DV], F32, name="o", bufs=1)
+            for i in range(TILES):
+                nc.tensor.matmul_mx(
+                    out=o[:, i, :],
+                    lhsT=codes[:, i * P : (i + 1) * P].bitcast(FP8X4),
+                    lhsT_scale=scales[:, i * P : (i + 1) * P],
+                    rhs=v_codes[:, h, :].bitcast(FP8X4),
+                    rhs_scale=v_scales[:, h, :],
+                    start=True,
+                    stop=True,
+                )
+            live["o", j] = o
+
+        def copy_o(j):
+            y = work.tile([P, TILES, DV], F32, align_bytes=64, name="y")
+            nc.scalar.copy(out=y[:], in_=live["o", j][:])
+            nc.sync.dma_start(out=out_view[j], in_=y[:])
+
+        def head_prep(h, part, state):
+            if part == 0:
+                state["kg"] = keep.tile([P, 2, 1024], BF16, align_bytes=64, name="k_grouped%d" % h)
+                ps = k_transposes(h, 0, "flip_b" if h == 0 else "flip_q")
+                k_copy(h, 0, ps, state["kg"], nc.scalar.copy)
+            elif part == 1:
+                ps = k_transposes(h, 1, "o" if h == 0 else "flip_q")
+                k_copy(h, 1, ps, state["kg"], nc.vector.tensor_copy if h == 0 else nc.scalar.copy)
+            elif part == 2:
+                k_quant(h, state["kg"])
+            elif part == 3:
+                state["vg"] = v_group(h)
+                if h == 0:
+                    v_quant(h, state["vg"])
+            elif part == 4:
+                gains(h)
+
+        warm = keep.tile([P, 1], F32)
+        nc.scalar.activation(out=warm[:], in_=ident[:, 0:1], func=ACTF.Exp)
+        h0, h1 = {}, {}
+
+        def ok(j):
+            return 0 <= j < PAIRS
+
+        def mid(i):
+            if i in (4, 5):
+                head_prep(1, i - 4, h1)
+            if i == 6:
+                head_prep(1, 2, h1)
+            if i == 7:
+                head_prep(1, 3, h1)
+            if i == 8:
+                gains(1)
+                v_quant(1, h1["vg"])
+            if i == -1:
+                gain_flip(0)
+                gain_to_psum(0)
+            if i == 10:
+                gain_flip(1)
+
+        for i in range(-6, PAIRS + 4):
+            if i == PAIRS_PER_HEAD:
+                gain_to_psum(1)
+            if ok(i + 5):
+                scale_q0(i + 5)
+            if ok(i - 2):
+                outputs(i - 2)
+            if ok(i - 1):
+                copy_b(i - 1)
+            if ok(i + 2):
+                quant_q(i + 2)
+            if ok(i):
+                recips(i)
+            if ok(i + 1):
+                maxima(i + 1, 0)
+            if ok(i + 5):
+                cast_q(i + 5)
+            if ok(i + 3):
+                copy_q(i + 3)
+            mid(i)
+            if ok(i + 2):
+                scores(i + 2)
+            if ok(i + 1):
+                maxima(i + 1, 1)
+            if ok(i - 2):
+                copy_o(i - 2)
+            if ok(i + 4):
+                scale_q1(i + 4)
+            if ok(i + 4):
+                flip_q(i + 4)
+            if ok(i + 1):
+                biases(i + 1)
+            if ok(i):
+                norms(i, 0)
+            if ok(i + 5):
+                hold(i + 5)
+            if ok(i):
+                norms(i, 1)
+            if ok(i):
+                flip_b(i)
+            if ok(i + 1):
+                exps(i + 1, 1)
+            if ok(i - 1):
+                quant_b(i - 1)
+            if ok(i + 1):
+                exps(i + 1, 0)
+            if i == -5:
+                head_prep(0, 0, h0)
+                head_prep(0, 1, h0)
+            if i == -4:
+                head_prep(0, 2, h0)
+            if i == -2:
+                nc.scalar.activation(out=tg[:], in_=g_raw[:], func=ACTF.Tanh)
+                head_prep(0, 4, h0)
+                head_prep(0, 3, h0)

@@ -30,7 +30,7 @@ def tile_llamaadaptergatedpromptattention_t_kernel(tc, q_bytes, q_scale, k, v, g
     nc = tc.nc
     with ExitStack() as ctx:
         keep = ctx.enter_context(tc.tile_pool(name="keep", bufs=1))
-        work = ctx.enter_context(tc.tile_pool(name="work", bufs=5))
+        work = ctx.enter_context(tc.tile_pool(name="work", bufs=6))
         psum = ctx.enter_context(tc.psum_pool(name="psum", bufs=1))
         ctx.enter_context(tc.manual_schedule())
 
@@ -313,6 +313,9 @@ def tile_llamaadaptergatedpromptattention_t_kernel(tc, q_bytes, q_scale, k, v, g
             return 0 <= j < PAIRS
 
         def mid(i):
+            if i == -1:
+                gain_flip(0)
+                gain_to_psum(0)
             if i in (4, 5):
                 head_prep(1, i - 4, h1)
             if i == 6:
@@ -322,64 +325,62 @@ def tile_llamaadaptergatedpromptattention_t_kernel(tc, q_bytes, q_scale, k, v, g
             if i == 8:
                 gains(1)
                 v_quant(1, h1["vg"])
-            if i == -1:
-                gain_flip(0)
-                gain_to_psum(0)
             if i == 10:
                 gain_flip(1)
-
-        for i in range(-6, PAIRS + 4):
             if i == PAIRS_PER_HEAD:
                 gain_to_psum(1)
-            if ok(i + 5):
-                scale_q0(i + 5)
-            if ok(i - 2):
-                outputs(i - 2)
-            if ok(i - 1):
-                copy_b(i - 1)
-            if ok(i + 2):
-                quant_q(i + 2)
-            if ok(i):
-                recips(i)
-            if ok(i + 1):
-                maxima(i + 1, 0)
-            if ok(i + 5):
-                cast_q(i + 5)
-            if ok(i + 3):
-                copy_q(i + 3)
-            mid(i)
+
+        for i in range(-7, PAIRS + 3):
             if ok(i + 2):
                 scores(i + 2)
-            if ok(i + 1):
-                maxima(i + 1, 1)
-            if ok(i - 2):
-                copy_o(i - 2)
-            if ok(i + 4):
-                scale_q1(i + 4)
-            if ok(i + 4):
-                flip_q(i + 4)
+            if ok(i - 1):
+                norms(i - 1, 1)
             if ok(i + 1):
                 biases(i + 1)
-            if ok(i):
-                norms(i, 0)
+            if ok(i + 4):
+                copy_q(i + 4)
+            mid(i)
+            if ok(i - 2):
+                quant_b(i - 2)
+            if ok(i + 6):
+                cast_q(i + 6)
+            if ok(i + 1):
+                exps(i + 1, 0)
+            if ok(i + 7):
+                scale_q0(i + 7)
             if ok(i + 5):
-                hold(i + 5)
-            if ok(i):
-                norms(i, 1)
-            if ok(i):
-                flip_b(i)
+                flip_q(i + 5)
+            if ok(i + 4):
+                quant_q(i + 4)
             if ok(i + 1):
                 exps(i + 1, 1)
             if ok(i - 1):
-                quant_b(i - 1)
-            if ok(i + 1):
-                exps(i + 1, 0)
-            if i == -5:
+                flip_b(i - 1)
+            if ok(i + 2):
+                maxima(i + 2, 0)
+            if ok(i):
+                recips(i)
+            if ok(i + 2):
+                maxima(i + 2, 1)
+            if ok(i - 2):
+                outputs(i - 2)
+            if ok(i):
+                norms(i, 0)
+            if ok(i + 7):
+                hold(i + 7)
+            if ok(i + 6):
+                scale_q1(i + 6)
+            if ok(i - 1):
+                copy_b(i - 1)
+            if ok(i - 2):
+                copy_o(i - 2)
+            if i == -6:
                 head_prep(0, 0, h0)
                 head_prep(0, 1, h0)
-            if i == -4:
+            if i == -5:
                 head_prep(0, 2, h0)
-            if i == -2:
+            if i == -3:
                 nc.scalar.activation(out=tg[:], in_=g_raw[:], func=ACTF.Tanh)
                 head_prep(0, 4, h0)
+            if i == 0:
                 head_prep(0, 3, h0)

@@ -23,6 +23,7 @@ PAIR = TILES * P
 PAIRS_PER_HEAD = T // PAIR
 PAIRS = H * PAIRS_PER_HEAD
 ROOT = 512.0 ** -0.5
+LEAD = 4
 SEG = ((0, 64), (64, 256))
 
 
@@ -55,13 +56,13 @@ def tile_llamaadaptergatedpromptattention_t_kernel(tc, q_bytes, q_scale, k, v, g
 
         load_q(0, 1)
         nc.sync.dma_start(out=qs[:], in_=q_scale.rearrange("a b e -> (a b e)").partition_broadcast(P))
-        nc.sync.dma_start(out=k_raw[:, 0, :, :], in_=k[0].rearrange("(r j) e -> r j e", j=4))
         load_q(1, 2)
-        nc.sync.dma_start(out=v_raw[:, 0, :, :], in_=v[0].rearrange("(p t) d -> p t d", t=4))
+        nc.sync.dma_start(out=k_raw[:, 0, :, :], in_=k[0].rearrange("(r j) e -> r j e", j=4))
+        load_q(2, 4)
         nc.sync.dma_start(out=g_raw[:], in_=gate.partition_broadcast(P))
         nc.sync.dma_start(out=c_raw[:].rearrange("p h n -> p (h n)"), in_=c.rearrange("h n -> (h n)").partition_broadcast(P))
-        load_q(2, 4)
         load_q(4, 8)
+        nc.sync.dma_start(out=v_raw[:, 0, :, :], in_=v[0].rearrange("(p t) d -> p t d", t=4))
         nc.sync.dma_start(out=k_raw[:, 1, :, :], in_=k[1].rearrange("(r j) e -> r j e", j=4))
         nc.sync.dma_start(out=v_raw[:, 1, :, :], in_=v[1].rearrange("(p t) d -> p t d", t=4))
         load_q(8, 16)
@@ -111,14 +112,10 @@ def tile_llamaadaptergatedpromptattention_t_kernel(tc, q_bytes, q_scale, k, v, g
         def gains(h):
             src = c_raw[:, h, :].rearrange("p (x u e) -> p u x e", u=2, e=2)
             dst = gain[:, h].rearrange("p u (x e) -> p u x e", e=2)
-            nc.gpsimd.tensor_scalar(
-                out=dst[:, :, 0:32, :], in0=src[:, :, 0:32, :], scalar1=tg[:, h : h + 1], scalar2=1.0,
-                op0=ALU.mult, op1=ALU.mult,
+            nc.scalar.activation(
+                out=dst[:, :, 0:32, :], in_=src[:, :, 0:32, :], func=ACTF.Copy, scale=tg[:, h : h + 1]
             )
-            nc.gpsimd.tensor_scalar(
-                out=dst[:, :, 32:128, :], in0=src[:, :, 32:128, :], scalar1=1.0, scalar2=1.0,
-                op0=ALU.mult, op1=ALU.mult,
-            )
+            nc.scalar.copy(out=dst[:, :, 32:128, :], in_=src[:, :, 32:128, :])
 
         live = {}
 
@@ -139,27 +136,29 @@ def tile_llamaadaptergatedpromptattention_t_kernel(tc, q_bytes, q_scale, k, v, g
             live["c", h] = cp
 
         def cast_q(j):
+            if j < LEAD:
+                return
             qc = work.tile([P, E], BF16, align_bytes=64, name="q_cast")
             nc.scalar.copy(out=qc[:], in_=q_raw[:, j * row + E : (j + 1) * row].bitcast(FP8))
             live["cast", j] = qc
 
         def scale_q0(j):
-            q0 = work.tile([P, E], BF16, align_bytes=64, name="q_plain0")
-            nc.vector.tensor_tensor(
-                out=q0[:], in0=q_raw[:, j * row : j * row + E].bitcast(FP8), in1=qs[:], op=ALU.mult,
-            )
-            live["qb", j, 0] = q0
+            for i in range(TILES if j < LEAD else 1):
+                qb = work.tile([P, E], BF16, align_bytes=64, name="q_plain%d" % i)
+                a = j * row + i * E
+                nc.vector.tensor_tensor(out=qb[:], in0=q_raw[:, a : a + E].bitcast(FP8), in1=qs[:], op=ALU.mult)
+                live["qb", j, i] = qb
 
         def hold(j):
-            held = work.tile([P, 1], BF16, name="held")
-            nc.gpsimd.tensor_scalar(
-                out=held[:], in0=live["qb", j, 0][:, 0:1], scalar1=1.0, scalar2=1.0, op0=ALU.mult, op1=ALU.mult
-            )
+            held = work.tile([P, 1], U32, name="held")
+            nc.gpsimd.tensor_copy(out=held[:], in_=live["qc", j][0][:, 0:1])
 
         def scale_q1(j):
-            q1 = work.tile([P, E], BF16, align_bytes=64, name="q_plain1")
-            nc.gpsimd.tensor_tensor(out=q1[:], in0=live["cast", j][:], in1=qs[:], op=ALU.mult)
-            live["qb", j, 1] = q1
+            if j < LEAD:
+                return
+            qb = work.tile([P, E], BF16, align_bytes=64, name="q_plain1")
+            nc.gpsimd.tensor_tensor(out=qb[:], in0=live["cast", j][:], in1=qs[:], op=ALU.mult)
+            live["qb", j, 1] = qb
 
         def flip_q(j):
             ps = psum.tile([P, 2, 2, P], F32, name="flip_q", bufs=1)
@@ -200,7 +199,7 @@ def tile_llamaadaptergatedpromptattention_t_kernel(tc, q_bytes, q_scale, k, v, g
                 live["z", j, i] = z
 
         def maxima(j, i):
-            if i == 0:
+            if ("m", j) not in live:
                 live["m", j] = work.tile([P, 2 * TILES], F32, name="row_max")
             m = live["m", j]
             for s, (a, b) in enumerate(SEG):
@@ -295,7 +294,7 @@ def tile_llamaadaptergatedpromptattention_t_kernel(tc, q_bytes, q_scale, k, v, g
                 k_copy(h, 0, ps, state["kg"], nc.scalar.copy)
             elif part == 1:
                 ps = k_transposes(h, 1, "o" if h == 0 else "flip_q")
-                k_copy(h, 1, ps, state["kg"], nc.vector.tensor_copy if h == 0 else nc.scalar.copy)
+                k_copy(h, 1, ps, state["kg"], nc.scalar.copy)
             elif part == 2:
                 k_quant(h, state["kg"])
             elif part == 3:
@@ -327,60 +326,60 @@ def tile_llamaadaptergatedpromptattention_t_kernel(tc, q_bytes, q_scale, k, v, g
                 v_quant(1, h1["vg"])
             if i == 10:
                 gain_flip(1)
-            if i == PAIRS_PER_HEAD:
-                gain_to_psum(1)
 
         for i in range(-7, PAIRS + 3):
-            if ok(i + 2):
-                scores(i + 2)
-            if ok(i - 1):
-                norms(i - 1, 1)
+            if i == PAIRS_PER_HEAD + 2:
+                gain_to_psum(1)
+            if ok(i + 7):
+                cast_q(i + 7)
             if ok(i + 1):
                 biases(i + 1)
             if ok(i + 4):
+                flip_q(i + 4)
+            if ok(i - 2):
+                norms(i - 2, 0)
+            if ok(i - 2):
+                norms(i - 2, 1)
+            if ok(i + 2):
+                scores(i + 2)
+            if ok(i + 4):
                 copy_q(i + 4)
             mid(i)
+            if ok(i - 3):
+                quant_b(i - 3)
             if ok(i - 2):
-                quant_b(i - 2)
-            if ok(i + 6):
-                cast_q(i + 6)
-            if ok(i + 1):
-                exps(i + 1, 0)
+                flip_b(i - 2)
+            if ok(i - 1):
+                recips(i - 1)
+            if ok(i - 3):
+                outputs(i - 3)
+            if ok(i + 3):
+                quant_q(i + 3)
             if ok(i + 7):
                 scale_q0(i + 7)
-            if ok(i + 5):
-                flip_q(i + 5)
-            if ok(i + 4):
-                quant_q(i + 4)
-            if ok(i + 1):
-                exps(i + 1, 1)
-            if ok(i - 1):
-                flip_b(i - 1)
-            if ok(i + 2):
-                maxima(i + 2, 0)
-            if ok(i):
-                recips(i)
             if ok(i + 2):
                 maxima(i + 2, 1)
+            if ok(i + 3):
+                hold(i + 3)
+            if ok(i + 1):
+                exps(i + 1, 1)
+            if ok(i + 1):
+                exps(i + 1, 0)
             if ok(i - 2):
-                outputs(i - 2)
-            if ok(i):
-                norms(i, 0)
-            if ok(i + 7):
-                hold(i + 7)
+                copy_b(i - 2)
+            if ok(i + 2):
+                maxima(i + 2, 0)
             if ok(i + 6):
                 scale_q1(i + 6)
-            if ok(i - 1):
-                copy_b(i - 1)
-            if ok(i - 2):
-                copy_o(i - 2)
-            if i == -6:
+            if ok(i - 3):
+                copy_o(i - 3)
+            if i == -7:
                 head_prep(0, 0, h0)
                 head_prep(0, 1, h0)
-            if i == -5:
+            if i == -6:
                 head_prep(0, 2, h0)
-            if i == -3:
+            if i == -4:
                 nc.scalar.activation(out=tg[:], in_=g_raw[:], func=ACTF.Tanh)
                 head_prep(0, 4, h0)
-            if i == 0:
+            if i == -1:
                 head_prep(0, 3, h0)

from contextlib import ExitStack

import concourse.mybir as mybir
from concourse.masks import make_identity

H, T, E, L, S, DV = 2, 4096, 512, 128, 384, 256
N = L + S
P = 128
FLOPS = 2 * H * T * N * (E + DV)

F32 = mybir.dt.float32
BF16 = mybir.dt.bfloat16
U32 = mybir.dt.uint32
U8 = mybir.dt.uint8
FP8 = mybir.dt.float8_e4m3fn
FP8X4 = mybir.dt.float8_e4m3fn_x4
ALU = mybir.AluOpType
ACTF = mybir.ActivationFunctionType
AX = mybir.AxisListType

TILES = 2
PAIR = TILES * P
PAIRS_PER_HEAD = T // PAIR
PAIRS = H * PAIRS_PER_HEAD
ROOT = 512.0 ** -0.5
LEAD = 4
SEG = ((0, 64), (64, 256))


def tile_llamaadaptergatedpromptattention_t_kernel(tc, q_bytes, q_scale, k, v, gate, c, out):
    nc = tc.nc
    with ExitStack() as ctx:
        keep = ctx.enter_context(tc.tile_pool(name="keep", bufs=1))
        work = ctx.enter_context(tc.tile_pool(name="work", bufs=6))
        psum = ctx.enter_context(tc.psum_pool(name="psum", bufs=1))
        ctx.enter_context(tc.manual_schedule())

        ident = keep.tile([P, P], F32)
        make_identity(nc, ident[:])

        q_raw = keep.tile([P, PAIRS * TILES * E], U8, align_bytes=64)
        qs = keep.tile([P, E], F32, align_bytes=64)
        k_raw = keep.tile([P, H, 4, E], BF16, align_bytes=64)
        v_raw = keep.tile([P, H, 4, DV], BF16, align_bytes=64)
        c_raw = keep.tile([P, H, N], BF16, align_bytes=64)
        g_raw = keep.tile([P, H], BF16, align_bytes=64)
        q_view = q_bytes.rearrange("h (j p i) e -> p (h j) (i e)", p=P, i=TILES)
        out_view = out.rearrange("h (j p i) d -> (h j) p i d", p=P, i=TILES)
        row = TILES * E

        def load_q(a, b):
            nc.sync.dma_start(
                out=q_raw[:, a * row : b * row].rearrange("p (j x) -> p j x", x=row),
                in_=q_view[:, a:b, :],
            )

        load_q(0, 1)
        nc.sync.dma_start(out=qs[:], in_=q_scale.rearrange("a b e -> (a b e)").partition_broadcast(P))
        load_q(1, 2)
        nc.sync.dma_start(out=k_raw[:, 0, :, :], in_=k[0].rearrange("(r j) e -> r j e", j=4))
        load_q(2, 4)
        nc.sync.dma_start(out=g_raw[:], in_=gate.partition_broadcast(P))
        nc.sync.dma_start(out=c_raw[:].rearrange("p h n -> p (h n)"), in_=c.rearrange("h n -> (h n)").partition_broadcast(P))
        load_q(4, 8)
        nc.sync.dma_start(out=v_raw[:, 0, :, :], in_=v[0].rearrange("(p t) d -> p t d", t=4))
        nc.sync.dma_start(out=k_raw[:, 1, :, :], in_=k[1].rearrange("(r j) e -> r j e", j=4))
        nc.sync.dma_start(out=v_raw[:, 1, :, :], in_=v[1].rearrange("(p t) d -> p t d", t=4))
        load_q(8, 16)
        load_q(16, 24)
        load_q(24, 32)

        tg = keep.tile([P, H], F32)
        gain = keep.tile([P, H, 2, 256], F32, align_bytes=64)
        k_codes = keep.tile([P, H, N], U32, align_bytes=64)
        k_scales = keep.tile([P, H, N], U8, align_bytes=64)
        v_codes = keep.tile([P, H, DV], U32, align_bytes=64)
        v_scales = keep.tile([P, H, DV], U8, align_bytes=64)

        def k_transposes(h, w, bank):
            ps = psum.tile([P, 2, 2, P], F32, name=bank, bufs=1)
            for e in range(2):
                words = k_raw[:, h, 2 * w + e, :].bitcast(F32)
                for u in range(2):
                    nc.tensor.transpose(ps[:, e, u, :], words[:, u : 256 : 2], ident[:])
            return ps

        def k_copy(h, w, ps, kg, engine):
            engine(
                out=kg[:, w].bitcast(F32).rearrange("p (r e u) -> p r e u", e=2, u=2),
                in_=ps[:].rearrange("p e u r -> p r e u"),
            )

        def k_quant(h, kg):
            nc.vector.quantize_mx(
                out=k_codes[:, h, :].bitcast(FP8X4),
                scales=k_scales[:, h, :],
                in_=kg[:].rearrange("p w x -> p (w x)"),
            )

        def v_group(h):
            vg = keep.tile([P, DV, 4], BF16, align_bytes=64, name="v_grouped%d" % h)
            nc.vector.tensor_copy(out=vg[:], in_=v_raw[:, h].rearrange("p t d -> p d t"))
            return vg

        def v_quant(h, vg):
            nc.vector.quantize_mx(
                out=v_codes[:, h, :].bitcast(FP8X4),
                scales=v_scales[:, h, :],
                in_=vg[:].rearrange("p d t -> p (d t)"),
            )

        def gains(h):
            src = c_raw[:, h, :].rearrange("p (x u e) -> p u x e", u=2, e=2)
            dst = gain[:, h].rearrange("p u (x e) -> p u x e", e=2)
            nc.scalar.activation(
                out=dst[:, :, 0:32, :], in_=src[:, :, 0:32, :], func=ACTF.Copy, scale=tg[:, h : h + 1]
            )
            nc.scalar.copy(out=dst[:, :, 32:128, :], in_=src[:, :, 32:128, :])

        live = {}

        def gain_flip(h):
            ps = psum.tile([P, 4, P], F32, name="flip_q", bufs=1)
            flat = gain[:, h].rearrange("p u x -> p (u x)")
            for g in range(4):
                nc.tensor.transpose(ps[:, g, :], flat[:, g * P : (g + 1) * P], ident[:])
            gt = keep.tile([P, 4, P], F32, name="gain_turned%d" % h)
            nc.scalar.copy(out=gt[:], in_=ps[:])
            live["gt", h] = gt

        def gain_to_psum(h):
            cp = psum.tile([P, 2, 256], F32, name="c", bufs=1)
            flat = cp[:].rearrange("p u x -> p (u x)")
            for g in range(4):
                nc.tensor.transpose(flat[:, g * P : (g + 1) * P], live["gt", h][:, g, :], ident[:])
            live["c", h] = cp

        def cast_q(j):
            if j < LEAD:
                return
            qc = work.tile([P, E], BF16, align_bytes=64, name="q_cast")
            nc.scalar.copy(out=qc[:], in_=q_raw[:, j * row + E : (j + 1) * row].bitcast(FP8))
            live["cast", j] = qc

        def scale_q0(j):
            for i in range(TILES if j < LEAD else 1):
                qb = work.tile([P, E], BF16, align_bytes=64, name="q_plain%d" % i)
                a = j * row + i * E
                nc.vector.tensor_tensor(out=qb[:], in0=q_raw[:, a : a + E].bitcast(FP8), in1=qs[:], op=ALU.mult)
                live["qb", j, i] = qb

        def hold(j):
            held = work.tile([P, 1], U32, name="held")
            nc.gpsimd.tensor_copy(out=held[:], in_=live["qc", j][0][:, 0:1])

        def scale_q1(j):
            if j < LEAD:
                return
            qb = work.tile([P, E], BF16, align_bytes=64, name="q_plain1")
            nc.gpsimd.tensor_tensor(out=qb[:], in0=live["cast", j][:], in1=qs[:], op=ALU.mult)
            live["qb", j, 1] = qb

        def flip_q(j):
            ps = psum.tile([P, 2, 2, P], F32, name="flip_q", bufs=1)
            for i in range(TILES):
                words = live["qb", j, i][:].bitcast(F32)
                for u in range(2):
                    nc.tensor.transpose(ps[:, i, u, :], words[:, u : 256 : 2], ident[:])
            live["tq", j] = ps

        def copy_q(j):
            qg = work.tile([P, PAIR * 4], BF16, align_bytes=64, name="q_grouped")
            nc.scalar.copy(
                out=qg[:].bitcast(F32).rearrange("p (i r u) -> p i r u", i=TILES, u=2),
                in_=live["tq", j][:].rearrange("p i u r -> p i r u"),
            )
            live["qg", j] = qg

        def quant_q(j):
            codes = work.tile([P, PAIR], U32, align_bytes=64, name="q_codes")
            scales = work.tile([P, PAIR], U8, align_bytes=64, name="q_scales")
            nc.vector.quantize_mx(out=codes[:].bitcast(FP8X4), scales=scales[:], in_=live["qg", j][:])
            live["qc", j] = (codes, scales)

        def scores(j):
            h = j // PAIRS_PER_HEAD
            codes, scales = live["qc", j]
            for i in range(TILES):
                z = psum.tile([P, 2, 256], F32, name="z", bufs=4)
                nc.tensor.matmul_mx(
                    out=z[:].rearrange("p u x -> p (u x)"),
                    lhsT=codes[:, i * P : (i + 1) * P].bitcast(FP8X4),
                    lhsT_scale=scales[:, i * P : (i + 1) * P],
                    rhs=k_codes[:, h, :].bitcast(FP8X4),
                    rhs_scale=k_scales[:, h, :],
                    start=True,
                    stop=True,
                )
                live["z", j, i] = z

        def maxima(j, i):
            if ("m", j) not in live:
                live["m", j] = work.tile([P, 2 * TILES], F32, name="row_max")
            m = live["m", j]
            for s, (a, b) in enumerate(SEG):
                nc.vector.tensor_reduce(
                    out=m[:, 2 * i + s : 2 * i + s + 1], in_=live["z", j, i][:, :, a:b], axis=AX.XY, op=ALU.max
                )

        def biases(j):
            nb = work.tile([P, 2 * TILES], F32, name="neg_max")
            nc.gpsimd.tensor_scalar(
                out=nb[:], in0=live["m", j][:], scalar1=-ROOT, scalar2=1.0, op0=ALU.mult, op1=ALU.mult
            )
            live["nb", j] = nb

        def exps(j, i):
            if ("sums", j) not in live:
                live["sums", j] = work.tile([P, 2 * TILES], F32, name="row_sum")
            sums = live["sums", j]
            nb = live["nb", j]
            ex = work.tile([P, 2, 256], F32, align_bytes=64, name="ex%d" % i)
            for s, (a, b) in enumerate(SEG):
                col = slice(2 * i + s, 2 * i + s + 1)
                nc.scalar.activation(
                    out=ex[:, :, a:b], in_=live["z", j, i][:, :, a:b], func=ACTF.Exp,
                    bias=nb[:, col], scale=ROOT, accum_out=sums[:, col],
                )
            live["ex", j, i] = ex

        def recips(j):
            r = work.tile([P, 2 * TILES], F32, name="recip")
            nc.vector.reciprocal(out=r[:], in_=live["sums", j][:])
            live["r", j] = r

        def norms(j, i):
            h = j // PAIRS_PER_HEAD
            bb = work.tile([P, 2, 256], BF16, align_bytes=64, name="b_plain%d" % i)
            for s, (a, b) in enumerate(SEG):
                nc.vector.scalar_tensor_tensor(
                    out=bb[:, :, a:b], in0=live["ex", j, i][:, :, a:b],
                    scalar=live["r", j][:, 2 * i + s : 2 * i + s + 1],
                    in1=live["c", h][:, :, a:b], op0=ALU.mult, op1=ALU.mult,
                )
            live["bb", j, i] = bb

        def flip_b(j):
            ps = psum.tile([P, 2, 2, P], F32, name="flip_b", bufs=1)
            for i in range(TILES):
                words = live["bb", j, i][:].rearrange("p u x -> p (u x)").bitcast(F32)
                for u in range(2):
                    nc.tensor.transpose(ps[:, i, u, :], words[:, 128 * u : 128 * (u + 1)], ident[:])
            live["tb", j] = ps

        def copy_b(j):
            bg = work.tile([P, PAIR * 4], BF16, align_bytes=64, name="b_grouped")
            nc.scalar.copy(
                out=bg[:].bitcast(F32).rearrange("p (i r u) -> p i r u", i=TILES, u=2),
                in_=live["tb", j][:].rearrange("p i u r -> p i r u"),
            )
            live["bg", j] = bg

        def quant_b(j):
            codes = work.tile([P, PAIR], U32, align_bytes=64, name="b_codes")
            scales = work.tile([P, PAIR], U8, align_bytes=64, name="b_scales")
            nc.vector.quantize_mx(out=codes[:].bitcast(FP8X4), scales=scales[:], in_=live["bg", j][:])
            live["bc", j] = (codes, scales)

        def outputs(j):
            h = j // PAIRS_PER_HEAD
            codes, scales = live["bc", j]
            o = psum.tile([P, TILES, DV], F32, name="o", bufs=1)
            for i in range(TILES):
                nc.tensor.matmul_mx(
                    out=o[:, i, :],
                    lhsT=codes[:, i * P : (i + 1) * P].bitcast(FP8X4),
                    lhsT_scale=scales[:, i * P : (i + 1) * P],
                    rhs=v_codes[:, h, :].bitcast(FP8X4),
                    rhs_scale=v_scales[:, h, :],
                    start=True,
                    stop=True,
                )
            live["o", j] = o

        def copy_o(j):
            y = work.tile([P, TILES, DV], F32, align_bytes=64, name="y")
            nc.scalar.copy(out=y[:], in_=live["o", j][:])
            nc.sync.dma_start(out=out_view[j], in_=y[:])

        def head_prep(h, part, state):
            if part == 0:
                state["kg"] = keep.tile([P, 2, 1024], BF16, align_bytes=64, name="k_grouped%d" % h)
                ps = k_transposes(h, 0, "flip_b" if h == 0 else "flip_q")
                k_copy(h, 0, ps, state["kg"], nc.scalar.copy)
            elif part == 1:
                ps = k_transposes(h, 1, "o" if h == 0 else "flip_q")
                k_copy(h, 1, ps, state["kg"], nc.scalar.copy)
            elif part == 2:
                k_quant(h, state["kg"])
            elif part == 3:
                state["vg"] = v_group(h)
                if h == 0:
                    v_quant(h, state["vg"])
            elif part == 4:
                gains(h)

        warm = keep.tile([P, 1], F32)
        nc.scalar.activation(out=warm[:], in_=ident[:, 0:1], func=ACTF.Exp)
        h0, h1 = {}, {}

        def ok(j):
            return 0 <= j < PAIRS

        def mid(i):
            if i == -1:
                gain_flip(0)
                gain_to_psum(0)
            if i in (4, 5):
                head_prep(1, i - 4, h1)
            if i == 6:
                head_prep(1, 2, h1)
            if i == 7:
                head_prep(1, 3, h1)
            if i == 8:
                gains(1)
                v_quant(1, h1["vg"])
            if i == 10:
                gain_flip(1)

        for i in range(-7, PAIRS + 3):
            if i == PAIRS_PER_HEAD + 2:
                gain_to_psum(1)
            if ok(i + 7):
                cast_q(i + 7)
            if ok(i + 1):
                biases(i + 1)
            if ok(i + 4):
                flip_q(i + 4)
            if ok(i - 2):
                norms(i - 2, 0)
            if ok(i - 2):
                norms(i - 2, 1)
            if ok(i + 2):
                scores(i + 2)
            if ok(i + 4):
                copy_q(i + 4)
            mid(i)
            if ok(i - 3):
                quant_b(i - 3)
            if ok(i - 2):
                flip_b(i - 2)
            if ok(i - 1):
                recips(i - 1)
            if ok(i - 3):
                outputs(i - 3)
            if ok(i + 3):
                quant_q(i + 3)
            if ok(i + 7):
                scale_q0(i + 7)
            if ok(i + 2):
                maxima(i + 2, 1)
            if ok(i + 3):
                hold(i + 3)
            if ok(i + 1):
                exps(i + 1, 1)
            if ok(i + 1):
                exps(i + 1, 0)
            if ok(i - 2):
                copy_b(i - 2)
            if ok(i + 2):
                maxima(i + 2, 0)
            if ok(i + 6):
                scale_q1(i + 6)
            if ok(i - 3):
                copy_o(i - 3)
            if i == -7:
                head_prep(0, 0, h0)
                head_prep(0, 1, h0)
            if i == -6:
                head_prep(0, 2, h0)
            if i == -4:
                nc.scalar.activation(out=tg[:], in_=g_raw[:], func=ACTF.Tanh)
                head_prep(0, 4, h0)
            if i == -1:
                head_prep(0, 3, h0)
